import numpy as np
import ml_dtypes


def mxq(x, axis, fmt="e4m3"):
    dtype, down = {"e4m3": (ml_dtypes.float8_e4m3fn, 7), "e5m2": (ml_dtypes.float8_e5m2, 14)}[fmt]
    v = np.moveaxis(np.asarray(x, np.float32).astype(ml_dtypes.bfloat16).astype(np.float64), axis, -1)
    blocks = v.reshape(v.shape[:-1] + (-1, 32))
    amax = np.abs(blocks).max(-1, keepdims=True)
    byte = np.maximum(np.where(amax > 0, np.frexp(amax)[1] - 1 + 127, 0) - down, 1)
    scale = np.exp2(byte - 127.0)
    codes = (blocks / scale).astype(np.float32).astype(dtype).astype(np.float64)
    return np.moveaxis((codes * scale).reshape(v.shape), -1, axis)


WIDE = False


def mx_kscale(k):
    if not WIDE:
        return np.ones(k)
    levels = np.array([10, -10, 5, -5, 0])
    if k % 512:
        return np.exp2(np.random.permutation(np.resize(levels, k // 32))).repeat(32)
    a = np.empty((k // 512, 16))
    for p in range(k // 512):
        a[p, :8] = np.random.permutation(np.resize(levels, 8))
        for g in range(8):
            far = levels[np.abs(levels - a[p, g]) >= 10]
            a[p, g + 8] = far[np.random.randint(len(far))]
    return np.exp2(a.ravel()).repeat(32)


def f64(x):
    return np.asarray(x).astype(np.float64)


def striped(idx):
    return np.tile(np.asarray(idx).reshape(-1, 16).T, (8, 1)).astype(np.uint16)


def unstriped(offs):
    return offs[:16].T.reshape(-1).astype(np.int64)


E2M1 = np.array([0.0, 0.5, 1.0, 1.5, 2.0, 3.0, 4.0, 6.0, -0.0, -0.5, -1.0, -1.5, -2.0, -3.0, -4.0, -6.0])


def pack_weight(w, fmt):
    k, n = w.shape
    w = f64(np.asarray(w, np.float32).astype(ml_dtypes.bfloat16)).reshape(k // 32, 32, n)
    amax = np.abs(w).max(1)
    if fmt == "e4m3":
        byte = np.frexp(amax)[1] - 1 + 127 - 7
    else:
        mant, ex = np.frexp(amax / 6.0)
        byte = np.where(mant > 0.5, ex, ex - 1) + 127
    byte = np.clip(np.where(amax > 0, byte, 1), 1, 254)
    scaled = (w * np.exp2(127.0 - byte)[:, None, :]).reshape(k, n).astype(np.float32)
    by_word = np.ascontiguousarray(scaled.reshape(k // 512, 128, 4, n).transpose(0, 1, 3, 2))
    if fmt == "e4m3":
        words = by_word.astype(ml_dtypes.float8_e4m3fn).view(np.uint8)
    else:
        c = by_word.astype(ml_dtypes.float4_e2m1fn).view(np.uint8) & 0xF
        words = (c[..., 0::2] | (c[..., 1::2] << 4)).reshape(k // 512, 128, 2 * n)
    return np.ascontiguousarray(words), np.ascontiguousarray(byte.astype(np.uint8).reshape(k // 512, 16, n))


def unpack_weight(words, scales, fmt):
    g, _, n = scales.shape
    words = np.ascontiguousarray(words).reshape(g, 128, n, -1)
    if fmt == "e4m3":
        vals = words.view(ml_dtypes.float8_e4m3fn).astype(np.float64)
    else:
        nib = np.empty((g, 128, n, 4), np.uint8)
        nib[..., 0::2] = words & 0xF
        nib[..., 1::2] = words >> 4
        vals = E2M1[nib]
    vals = vals * np.repeat(np.exp2(scales.astype(np.float64) - 127.0), 8, axis=1)[..., None]
    return vals.transpose(0, 1, 3, 2).reshape(g * 512, n)


K, D, T, I, U = 512, 512, 1024, 256, 512


def setup_inputs():
    n = np.random.standard_normal
    idx = np.random.permutation(T)[:I]
    idx2 = np.random.permutation(U)[:I]
    fk = mx_kscale(K)
    tabp = pack_weight(n((K, T)) / fk[:, None], "e4m3")
    return {
        "mat": (n((K, D)) * 1 / np.sqrt(K) * fk[:, None]).astype(np.float32),
        "tab_words": tabp[0],
        "tab_scales": tabp[1],
        "coef": (np.random.uniform(-1.0, 1.0, (1, I))).astype(np.float32),
        "anchor": (n((D, U))).astype(np.float32),
        "pull": (np.random.uniform(0.1, 0.5, (1, I))).astype(np.float32),
        "old": (n((D, T)) * 0.5).astype(np.float32),
        "offs": striped(idx),
        "offs2": striped(idx2),
    }


def reference(mat, tab_words, tab_scales, coef, anchor, pull, old, offs, offs2):
    idx = unstriped(offs)
    idx2 = unstriped(offs2)
    tabu = unpack_weight(tab_words, tab_scales, "e4m3")
    matq = mxq(f64(mat), 0, "e4m3")
    tabidxg = tabu[:, idx]
    z = matq.T @ tabidxg
    g = z * f64(coef) + f64(anchor)[:, idx2] * f64(pull)
    gf = np.zeros((D, T))
    gf[:, idx] = g
    y = f64(old) + gf
    return y

@@ -1,0 +1,195 @@
+from contextlib import ExitStack
+
+import concourse.mybir as mybir
+from concourse.masks import make_identity
+
+K, D, T, I, U = 512, 512, 1024, 256, 512
+P = 128
+PACK = 4
+D_TILES = D // P
+HALF = D // 2
+
+F32 = mybir.dt.float32
+BF16 = mybir.dt.bfloat16
+I32 = mybir.dt.int32
+U32 = mybir.dt.uint32
+U16 = mybir.dt.uint16
+U8 = mybir.dt.uint8
+FP8X4 = mybir.dt.float8_e4m3fn_x4
+MULT = mybir.AluOpType.mult
+ADD = mybir.AluOpType.add
+
+FLOPS = 2 * K * D * I
+
+
+PE_TILES = 2
+BLOCKS = 4
+MAT_CHUNKS = ((0, 128), (128, 256), (256, 512))
+
+
+def tile_attend_gquadratic_kernel(tc, mat, tab_words, tab_scales, coef, anchor, pull, old, offs, offs2, out):
+    nc = tc.nc
+    with ExitStack() as ctx:
+        keep = ctx.enter_context(tc.tile_pool(name="keep", bufs=1))
+        shared = ctx.enter_context(tc.tile_pool(name="shared", bufs=1))
+        psum = ctx.enter_context(tc.psum_pool(name="psum", bufs=1))
+
+        offsets = keep.tile([P, I // 16], U16, name="offsets")
+        offsets2 = keep.tile([P, I // 16], U16, name="offsets2")
+        words = keep.tile([P, T], U32, name="words", align_bytes=64)
+        scale_bytes = keep.tile([P, T], U8, name="scale_bytes", align_bytes=64)
+        coef_cols = keep.tile([P, 2], F32, name="coef_cols")
+        pull_cols = keep.tile([P, 2], F32, name="pull_cols")
+        mat_raw = [keep.tile([P, PACK, b - a], F32, name=f"mat_raw{a}", tag=f"mat_raw{a}") for a, b in MAT_CHUNKS]
+        anchors = [keep.tile([P, U], F32, name=f"anchor{c}", align_bytes=64) for c in range(D_TILES)]
+        olds = [keep.tile([P, T], F32, name=f"old{c}") for c in range(D_TILES)]
+        windows = [keep.tile([P, T], F32, name=f"window{c}") for c in range(2)]
+        ident = keep.tile([P, P], F32, name="ident")
+
+        def rows(c):
+            return slice(c * P, (c + 1) * P)
+
+        nc.vector.memset(scale_bytes[:].bitcast(I32), 0)
+        mat_rows = mat.rearrange("(p j) d -> p j d", j=PACK)
+
+        def load_mat(n):
+            nc.sync.dma_start(mat_raw[n][:], mat_rows[:, :, MAT_CHUNKS[n][0] : MAT_CHUNKS[n][1]])
+
+        nc.sync.dma_start(offsets[:], offs)
+        nc.sync.dma_start(pull_cols[:], pull[0].rearrange("(p j) -> p j", j=2))
+        nc.sync.dma_start(offsets2[:], offs2)
+        nc.sync.dma_start(anchors[0][:], anchor[rows(0), :])
+        load_mat(0)
+        nc.sync.dma_start(words[:].bitcast(I32), tab_words[0].rearrange("p n t -> p (n t)").bitcast(I32))
+        for q in range(4):
+            nc.sync.dma_start(scale_bytes[32 * q : 32 * q + 4, :].bitcast(I32), tab_scales[0, 4 * q : 4 * q + 4, :].bitcast(I32))
+        nc.sync.dma_start(coef_cols[:], coef[0].rearrange("(p j) -> p j", j=2))
+        nc.sync.dma_start(anchors[1][:], anchor[rows(1), :])
+        load_mat(1)
+        nc.sync.dma_start(anchors[2][:], anchor[rows(2), :])
+        load_mat(2)
+        nc.sync.dma_start(olds[0][:], old[rows(0), :])
+        nc.sync.dma_start(anchors[3][:], anchor[rows(3), :])
+        nc.sync.dma_start(olds[1][:], old[rows(1), :])
+        nc.sync.dma_start(olds[2][:], old[rows(2), :])
+        nc.sync.dma_start(olds[3][:], old[rows(3), :])
+
+        make_identity(nc, ident[:])
+        for window in windows:
+            nc.vector.memset(window[:], 0.0)
+
+        def spread(cols, name, tag, copy):
+            bank = psum.tile([P, 2, P], F32, name=name + "_bank", tag=tag)
+            for j in range(2):
+                nc.tensor.transpose(bank[:, j, :], cols[:, j : j + 1].to_broadcast([P, P]), ident[:])
+            row = keep.tile([P, I], F32, name=name + "_row")
+            copy(row[:].rearrange("p (n j) -> p n j", j=2), bank[:].rearrange("p j n -> p n j"))
+            return row
+
+        pull_row = spread(pull_cols, "pull", "turned0", nc.vector.tensor_copy)
+        coef_row = spread(coef_cols, "coef", "turned1", nc.scalar.copy)
+
+        picked_words = keep.tile([P, I], U32, name="picked_words", tag="anchor0", align_bytes=64)
+        picked_scales = keep.tile([P, I], U8, name="picked_scales", tag="words", align_bytes=64)
+        pulled, weighted, stationary = {}, {}, {}
+
+        def quantise(n):
+            a, b = MAT_CHUNKS[n]
+            grouped = keep.tile([P, b - a, PACK], BF16, name=f"grouped{a}", tag=f"stage{n}", align_bytes=64)
+            nc.scalar.copy(
+                grouped[:].rearrange("p (c i) t -> p c t i", i=4),
+                mat_raw[n][:].rearrange("p t (c i) -> p c t i", i=4),
+            )
+            if n == 2:
+                codes = shared.tile([P, b - a], U32, name=f"codes{a}", offset=1536, align_bytes=64)
+            else:
+                codes = keep.tile([P, b - a], U32, name=f"codes{a}", tag="scale_bytes" if n == 0 else f"codes{a}", align_bytes=64)
+            scales = keep.tile([P, b - a], U8, name=f"scales{a}", align_bytes=64)
+            for c in range(a // P, b // P):
+                cols = slice(c * P - a, (c + 1) * P - a)
+                stationary[c] = (codes[:, cols], scales[:, cols])
+            nc.vector.quantize_mx(
+                out=codes[:].bitcast(FP8X4), scales=scales[:], in_=grouped[:].rearrange("p w t -> p (w t)")
+            )
+
+        def gather_anchor(c):
+            if c % 2 == 0:
+                pulled[c] = shared.tile([P, I], F32, name=f"pulled{c}", offset=2048 + 256 * c, align_bytes=64)
+            else:
+                pulled[c] = keep.tile([P, I], F32, name=f"pulled{c}", tag="stage2" if c == 3 else "pulled1", align_bytes=64)
+            nc.vector.tensor_tensor(pulled[c][:], anchors[c][:].indirect(offsets2[:]), pull_row[:], MULT)
+
+        def product(c):
+            z = psum.tile([P, I], F32, name=f"z{c}", tag=f"turned{c}" if c < 2 else f"z{c}")
+            nc.tensor.matmul_mx(
+                out=z[:],
+                lhsT=stationary[c][0].bitcast(FP8X4),
+                lhsT_scale=stationary[c][1],
+                rhs=picked_words[:].bitcast(FP8X4),
+                rhs_scale=picked_scales[:],
+                start=True,
+                stop=True,
+            )
+            weighted[c] = keep.tile([P, I], F32, name=f"weighted{c}", tag=f"weighted{(0, 0, 2, 3)[c]}", align_bytes=64)
+            nc.vector.tensor_tensor(weighted[c][:], z[:], coef_row[:], MULT)
+
+        def scatter(c):
+            nc.vector.tensor_tensor(windows[c % 2][:].indirect(offsets[:]), weighted[c][:], pulled[c][:], ADD)
+
+        def half(s):
+            return slice(s * (T // 2), (s + 1) * (T // 2))
+
+        def add_on_vector(c, s):
+            nc.vector.tensor_tensor(olds[c][:, half(s)], olds[c][:, half(s)], windows[c % 2][:, half(s)], ADD)
+            nc.sync.dma_start(out[rows(c), half(s)], olds[c][:, half(s)])
+
+        turned_banks = {}
+
+        def turn_old(c, s):
+            bank = psum.tile([P, BLOCKS, P], F32, name=f"turned{c}{s}", tag=f"turned{s}")
+            turned_banks[c, s] = bank
+            for j in range(BLOCKS):
+                nc.tensor.matmul(bank[:, j, :], olds[c][:, rows(BLOCKS * s + j)], ident[:], start=(j == 0), stop=False, is_transpose=True)
+
+        def add_on_tensor(c, s):
+            bank = turned_banks[c, s]
+            for j in range(BLOCKS):
+                nc.tensor.matmul(bank[:, j, :], windows[c % 2][:, rows(BLOCKS * s + j)], ident[:], start=False, stop=(j == BLOCKS - 1), is_transpose=True)
+            turned = keep.tile([P, BLOCKS, P], F32, name=f"turned_sum{c}{s}", tag="mat_raw256" if (c, s) == (0, 0) else f"turned_sum{c}{s}")
+            nc.scalar.copy(turned[:], bank[:])
+            back = psum.tile([P, BLOCKS, P], F32, name=f"back{c}{s}", tag=f"back{s}")
+            for j in range(BLOCKS):
+                nc.tensor.transpose(back[:, j, :], turned[:, j, :], ident[:])
+            result = keep.tile([P, BLOCKS, P], F32, name=f"result{c}{s}")
+            nc.scalar.copy(result[:], back[:])
+            nc.scalar.dma_start(out[rows(c), half(s)], result[:].rearrange("p j n -> p (j n)"))
+
+        gather_anchor(0)
+        nc.vector.tensor_copy(picked_words[:], words[:].indirect(offsets[:]))
+        nc.vector.tensor_copy(picked_scales[:], scale_bytes[:].indirect(offsets[:]))
+        quantise(0)
+        gather_anchor(1)
+        product(0)
+        quantise(1)
+        scatter(0)
+        product(1)
+        gather_anchor(2)
+        turn_old(0, 0)
+        turn_old(0, 1)
+        scatter(1)
+        quantise(2)
+        add_on_tensor(0, 0)
+        add_on_tensor(0, 1)
+        gather_anchor(3)
+        product(2)
+        scatter(2)
+        product(3)
+        turn_old(1, 0)
+        turn_old(1, 1)
+        add_on_tensor(1, 0)
+        add_on_tensor(1, 1)
+        add_on_vector(2, 0)
+        scatter(3)
+        add_on_vector(2, 1)
+        add_on_vector(3, 0)
+        add_on_vector(3, 1)

@@ -22,9 +22,19 @@ ADD = mybir.AluOpType.add
 FLOPS = 2 * K * D * I
 
 
-PE_TILES = 2
 BLOCKS = 4
 MAT_CHUNKS = ((0, 128), (128, 256), (256, 512))
+PLACES = {
+    "anchor0": 0, "picked_words": 0, "picked_scales": 1024, "codes0": 1280, "grouped1": 1792,
+    "words": 3072, "codes1": 3072, "pulled1": 3584, "grouped2": 4608, "pulled3": 3584,
+    "pulled0": 8192, "pulled2": 8192, "weighted0": 9216, "codes2": 9216,
+}
+BANKS = {
+    "pull": "a", "z1": "a", "turned01": "a", "turned11": "a",
+    "coef": "b", "z0": "b", "turned00": "b", "turned10": "b",
+    "z2": "c", "z3": "d",
+    "back00": "e", "back01": "f", "back10": "g", "back11": "h",
+}
 
 
 def tile_attend_gquadratic_kernel(tc, mat, tab_words, tab_scales, coef, anchor, pull, old, offs, offs2, out):
@@ -34,20 +44,28 @@ def tile_attend_gquadratic_kernel(tc, mat, tab_words, tab_scales, coef, anchor, 
         shared = ctx.enter_context(tc.tile_pool(name="shared", bufs=1))
         psum = ctx.enter_context(tc.psum_pool(name="psum", bufs=1))
 
-        offsets = keep.tile([P, I // 16], U16, name="offsets")
-        offsets2 = keep.tile([P, I // 16], U16, name="offsets2")
-        words = keep.tile([P, T], U32, name="words", align_bytes=64)
-        scale_bytes = keep.tile([P, T], U8, name="scale_bytes", align_bytes=64)
-        coef_cols = keep.tile([P, 2], F32, name="coef_cols")
-        pull_cols = keep.tile([P, 2], F32, name="pull_cols")
-        mat_raw = [keep.tile([P, PACK, b - a], F32, name=f"mat_raw{a}", tag=f"mat_raw{a}") for a, b in MAT_CHUNKS]
-        anchors = [keep.tile([P, U], F32, name=f"anchor{c}", align_bytes=64) for c in range(D_TILES)]
-        olds = [keep.tile([P, T], F32, name=f"old{c}") for c in range(D_TILES)]
-        windows = [keep.tile([P, T], F32, name=f"window{c}") for c in range(2)]
-        ident = keep.tile([P, P], F32, name="ident")
+        def place(name, shape, dtype):
+            if name in PLACES:
+                return shared.tile(shape, dtype, name=name, offset=PLACES[name], align_bytes=64)
+            return keep.tile(shape, dtype, name=name, align_bytes=64)
 
         def rows(c):
             return slice(c * P, (c + 1) * P)
+
+        def half(s):
+            return slice(s * (T // 2), (s + 1) * (T // 2))
+
+        offsets = keep.tile([P, I // 16], U16, name="offsets")
+        offsets2 = keep.tile([P, I // 16], U16, name="offsets2")
+        words = place("words", [P, T], U32)
+        scale_bytes = place("scale_bytes", [P, T], U8)
+        coef_cols = place("coef_cols", [P, 2], F32)
+        pull_cols = place("pull_cols", [P, 2], F32)
+        mat_raw = [place(f"mat_raw{n}", [P, PACK, b - a], F32) for n, (a, b) in enumerate(MAT_CHUNKS)]
+        anchors = [place(f"anchor{c}", [P, U], F32) for c in range(D_TILES)]
+        olds = [place(f"old{c}", [P, T], F32) for c in range(D_TILES)]
+        windows = [place(f"window{c}", [P, T], F32) for c in range(4)]
+        ident = place("ident", [P, P], F32)
 
         nc.vector.memset(scale_bytes[:].bitcast(I32), 0)
         mat_rows = mat.rearrange("(p j) d -> p j d", j=PACK)
@@ -55,98 +73,90 @@ def tile_attend_gquadratic_kernel(tc, mat, tab_words, tab_scales, coef, anchor, 
         def load_mat(n):
             nc.sync.dma_start(mat_raw[n][:], mat_rows[:, :, MAT_CHUNKS[n][0] : MAT_CHUNKS[n][1]])
 
+        def load_anchor(c):
+            nc.sync.dma_start(anchors[c][:], anchor[rows(c), :])
+
+        def load_old(c):
+            nc.sync.dma_start(olds[c][:], old[rows(c), :])
+
         nc.sync.dma_start(offsets[:], offs)
         nc.sync.dma_start(pull_cols[:], pull[0].rearrange("(p j) -> p j", j=2))
         nc.sync.dma_start(offsets2[:], offs2)
-        nc.sync.dma_start(anchors[0][:], anchor[rows(0), :])
+        load_anchor(0)
         load_mat(0)
         nc.sync.dma_start(words[:].bitcast(I32), tab_words[0].rearrange("p n t -> p (n t)").bitcast(I32))
         for q in range(4):
             nc.sync.dma_start(scale_bytes[32 * q : 32 * q + 4, :].bitcast(I32), tab_scales[0, 4 * q : 4 * q + 4, :].bitcast(I32))
         nc.sync.dma_start(coef_cols[:], coef[0].rearrange("(p j) -> p j", j=2))
-        nc.sync.dma_start(anchors[1][:], anchor[rows(1), :])
         load_mat(1)
-        nc.sync.dma_start(anchors[2][:], anchor[rows(2), :])
+        load_anchor(1)
+        load_old(0)
         load_mat(2)
-        nc.sync.dma_start(olds[0][:], old[rows(0), :])
-        nc.sync.dma_start(anchors[3][:], anchor[rows(3), :])
-        nc.sync.dma_start(olds[1][:], old[rows(1), :])
-        nc.sync.dma_start(olds[2][:], old[rows(2), :])
-        nc.sync.dma_start(olds[3][:], old[rows(3), :])
+        load_old(1)
+        load_anchor(2)
+        load_anchor(3)
+        load_old(2)
+        load_old(3)
 
         make_identity(nc, ident[:])
-        for window in windows:
-            nc.vector.memset(window[:], 0.0)
+        for c in range(len(windows)):
+            (nc.vector if c < 2 else nc.gpsimd).memset(windows[c][:], 0.0)
 
-        def spread(cols, name, tag, copy):
-            bank = psum.tile([P, 2, P], F32, name=name + "_bank", tag=tag)
+        def spread(cols, name, copy):
+            bank = psum.tile([P, 2, P], F32, name=name + "_bank", tag=BANKS[name])
             for j in range(2):
                 nc.tensor.transpose(bank[:, j, :], cols[:, j : j + 1].to_broadcast([P, P]), ident[:])
-            row = keep.tile([P, I], F32, name=name + "_row")
+            row = place(name + "_row", [P, I], F32)
             copy(row[:].rearrange("p (n j) -> p n j", j=2), bank[:].rearrange("p j n -> p n j"))
             return row
 
-        pull_row = spread(pull_cols, "pull", "turned0", nc.vector.tensor_copy)
-        coef_row = spread(coef_cols, "coef", "turned1", nc.scalar.copy)
+        pull_row = spread(pull_cols, "pull", nc.vector.tensor_copy)
+        coef_row = spread(coef_cols, "coef", nc.scalar.copy)
 
-        picked_words = keep.tile([P, I], U32, name="picked_words", tag="anchor0", align_bytes=64)
-        picked_scales = keep.tile([P, I], U8, name="picked_scales", tag="words", align_bytes=64)
-        pulled, weighted, stationary = {}, {}, {}
+        picked_words = place("picked_words", [P, I], U32)
+        picked_scales = place("picked_scales", [P, I], U8)
+        pulled, weighted, stationary, products, turned_banks, results = {}, {}, {}, {}, {}, {}
 
         def quantise(n):
             a, b = MAT_CHUNKS[n]
-            grouped = keep.tile([P, b - a, PACK], BF16, name=f"grouped{a}", tag=f"stage{n}", align_bytes=64)
+            grouped = place(f"grouped{n}", [P, b - a, PACK], BF16)
             nc.scalar.copy(
                 grouped[:].rearrange("p (c i) t -> p c t i", i=4),
                 mat_raw[n][:].rearrange("p t (c i) -> p c t i", i=4),
             )
-            if n == 2:
-                codes = shared.tile([P, b - a], U32, name=f"codes{a}", offset=1536, align_bytes=64)
-            else:
-                codes = keep.tile([P, b - a], U32, name=f"codes{a}", tag="scale_bytes" if n == 0 else f"codes{a}", align_bytes=64)
-            scales = keep.tile([P, b - a], U8, name=f"scales{a}", align_bytes=64)
+            codes = place(f"codes{n}", [P, b - a], U32)
+            scales = place(f"scales{n}", [P, b - a], U8)
+            nc.vector.quantize_mx(out=codes[:].bitcast(FP8X4), scales=scales[:], in_=grouped[:].rearrange("p w t -> p (w t)"))
             for c in range(a // P, b // P):
                 cols = slice(c * P - a, (c + 1) * P - a)
-                stationary[c] = (codes[:, cols], scales[:, cols])
-            nc.vector.quantize_mx(
-                out=codes[:].bitcast(FP8X4), scales=scales[:], in_=grouped[:].rearrange("p w t -> p (w t)")
-            )
+                products[c] = psum.tile([P, I], F32, name=f"z{c}", tag=BANKS[f"z{c}"])
+                nc.tensor.matmul_mx(
+                    out=products[c][:],
+                    lhsT=codes[:, cols].bitcast(FP8X4),
+                    lhsT_scale=scales[:, cols],
+                    rhs=picked_words[:].bitcast(FP8X4),
+                    rhs_scale=picked_scales[:],
+                    start=True,
+                    stop=True,
+                )
 
         def gather_anchor(c):
-            if c % 2 == 0:
-                pulled[c] = shared.tile([P, I], F32, name=f"pulled{c}", offset=2048 + 256 * c, align_bytes=64)
-            else:
-                pulled[c] = keep.tile([P, I], F32, name=f"pulled{c}", tag="stage2" if c == 3 else "pulled1", align_bytes=64)
+            pulled[c] = place(f"pulled{c}", [P, I], F32)
             nc.vector.tensor_tensor(pulled[c][:], anchors[c][:].indirect(offsets2[:]), pull_row[:], MULT)
 
-        def product(c):
-            z = psum.tile([P, I], F32, name=f"z{c}", tag=f"turned{c}" if c < 2 else f"z{c}")
-            nc.tensor.matmul_mx(
-                out=z[:],
-                lhsT=stationary[c][0].bitcast(FP8X4),
-                lhsT_scale=stationary[c][1],
-                rhs=picked_words[:].bitcast(FP8X4),
-                rhs_scale=picked_scales[:],
-                start=True,
-                stop=True,
-            )
-            weighted[c] = keep.tile([P, I], F32, name=f"weighted{c}", tag=f"weighted{(0, 0, 2, 3)[c]}", align_bytes=64)
-            nc.vector.tensor_tensor(weighted[c][:], z[:], coef_row[:], MULT)
+        def weigh(c):
+            weighted[c] = place(f"weighted{c}", [P, I], F32)
+            nc.vector.tensor_tensor(weighted[c][:], products[c][:], coef_row[:], MULT)
 
         def scatter(c):
-            nc.vector.tensor_tensor(windows[c % 2][:].indirect(offsets[:]), weighted[c][:], pulled[c][:], ADD)
-
-        def half(s):
-            return slice(s * (T // 2), (s + 1) * (T // 2))
+            nc.vector.tensor_tensor(windows[c % len(windows)][:].indirect(offsets[:]), weighted[c][:], pulled[c][:], ADD)
 
         def add_on_vector(c, s):
-            nc.vector.tensor_tensor(olds[c][:, half(s)], olds[c][:, half(s)], windows[c % 2][:, half(s)], ADD)
+            nc.vector.tensor_tensor(olds[c][:, half(s)], olds[c][:, half(s)], windows[c % len(windows)][:, half(s)], ADD)
             nc.sync.dma_start(out[rows(c), half(s)], olds[c][:, half(s)])
 
-        turned_banks = {}
-
         def turn_old(c, s):
-            bank = psum.tile([P, BLOCKS, P], F32, name=f"turned{c}{s}", tag=f"turned{s}")
+            bank = psum.tile([P, BLOCKS, P], F32, name=f"turned{c}{s}", tag=BANKS[f"turned{c}{s}"])
             turned_banks[c, s] = bank
             for j in range(BLOCKS):
                 nc.tensor.matmul(bank[:, j, :], olds[c][:, rows(BLOCKS * s + j)], ident[:], start=(j == 0), stop=False, is_transpose=True)
@@ -154,14 +164,15 @@ def tile_attend_gquadratic_kernel(tc, mat, tab_words, tab_scales, coef, anchor, 
         def add_on_tensor(c, s):
             bank = turned_banks[c, s]
             for j in range(BLOCKS):
-                nc.tensor.matmul(bank[:, j, :], windows[c % 2][:, rows(BLOCKS * s + j)], ident[:], start=False, stop=(j == BLOCKS - 1), is_transpose=True)
-            turned = keep.tile([P, BLOCKS, P], F32, name=f"turned_sum{c}{s}", tag="mat_raw256" if (c, s) == (0, 0) else f"turned_sum{c}{s}")
+                nc.tensor.matmul(bank[:, j, :], windows[c][:, rows(BLOCKS * s + j)], ident[:], start=False, stop=(j == BLOCKS - 1), is_transpose=True)
+            turned = place(f"turned_sum{c}{s}", [P, BLOCKS, P], F32)
             nc.scalar.copy(turned[:], bank[:])
-            back = psum.tile([P, BLOCKS, P], F32, name=f"back{c}{s}", tag=f"back{s}")
+            back = psum.tile([P, BLOCKS, P], F32, name=f"back{c}{s}", tag=BANKS[f"back{c}{s}"])
             for j in range(BLOCKS):
                 nc.tensor.transpose(back[:, j, :], turned[:, j, :], ident[:])
-            result = keep.tile([P, BLOCKS, P], F32, name=f"result{c}{s}")
+            result = place(f"result{c}{s}", [P, BLOCKS, P], F32)
             nc.scalar.copy(result[:], back[:])
+            results[c, s] = result
             nc.scalar.dma_start(out[rows(c), half(s)], result[:].rearrange("p j n -> p (j n)"))
 
         gather_anchor(0)
@@ -169,27 +180,27 @@ def tile_attend_gquadratic_kernel(tc, mat, tab_words, tab_scales, coef, anchor, 
         nc.vector.tensor_copy(picked_scales[:], scale_bytes[:].indirect(offsets[:]))
         quantise(0)
         gather_anchor(1)
-        product(0)
         quantise(1)
-        scatter(0)
-        product(1)
-        gather_anchor(2)
+        weigh(0)
+        weigh(1)
         turn_old(0, 0)
         turn_old(0, 1)
+        scatter(0)
         scatter(1)
         quantise(2)
         add_on_tensor(0, 0)
         add_on_tensor(0, 1)
+        gather_anchor(2)
         gather_anchor(3)
-        product(2)
+        weigh(2)
+        weigh(3)
         scatter(2)
-        product(3)
         turn_old(1, 0)
-        turn_old(1, 1)
         add_on_tensor(1, 0)
+        turn_old(1, 1)
         add_on_tensor(1, 1)
-        add_on_vector(2, 0)
         scatter(3)
+        add_on_vector(2, 0)
         add_on_vector(2, 1)
         add_on_vector(3, 0)
         add_on_vector(3, 1)

from contextlib import ExitStack

import concourse.mybir as mybir
from concourse.masks import make_identity

K, D, T, I, U = 512, 512, 1024, 256, 512
P = 128
PACK = 4
D_TILES = D // P
HALF = D // 2

F32 = mybir.dt.float32
BF16 = mybir.dt.bfloat16
I32 = mybir.dt.int32
U32 = mybir.dt.uint32
U16 = mybir.dt.uint16
U8 = mybir.dt.uint8
FP8X4 = mybir.dt.float8_e4m3fn_x4
MULT = mybir.AluOpType.mult
ADD = mybir.AluOpType.add

FLOPS = 2 * K * D * I


BLOCKS = 4
MAT_CHUNKS = ((0, 128), (128, 256), (256, 512))
PLACES = {
    "anchor0": 0, "picked_words": 0, "picked_scales": 1024, "codes0": 1280, "grouped1": 1792,
    "words": 3072, "codes1": 3072, "pulled1": 3584, "grouped2": 4608, "pulled3": 3584,
    "pulled0": 8192, "pulled2": 8192, "weighted0": 9216, "codes2": 9216,
}
BANKS = {
    "pull": "a", "z1": "a", "turned01": "a", "turned11": "a",
    "coef": "b", "z0": "b", "turned00": "b", "turned10": "b",
    "z2": "c", "z3": "d",
    "back00": "e", "back01": "f", "back10": "g", "back11": "h",
}


def tile_attend_gquadratic_kernel(tc, mat, tab_words, tab_scales, coef, anchor, pull, old, offs, offs2, out):
    nc = tc.nc
    with ExitStack() as ctx:
        keep = ctx.enter_context(tc.tile_pool(name="keep", bufs=1))
        shared = ctx.enter_context(tc.tile_pool(name="shared", bufs=1))
        psum = ctx.enter_context(tc.psum_pool(name="psum", bufs=1))

        def place(name, shape, dtype):
            if name in PLACES:
                return shared.tile(shape, dtype, name=name, offset=PLACES[name], align_bytes=64)
            return keep.tile(shape, dtype, name=name, align_bytes=64)

        def rows(c):
            return slice(c * P, (c + 1) * P)

        def half(s):
            return slice(s * (T // 2), (s + 1) * (T // 2))

        offsets = keep.tile([P, I // 16], U16, name="offsets")
        offsets2 = keep.tile([P, I // 16], U16, name="offsets2")
        words = place("words", [P, T], U32)
        scale_bytes = place("scale_bytes", [P, T], U8)
        coef_cols = place("coef_cols", [P, 2], F32)
        pull_cols = place("pull_cols", [P, 2], F32)
        mat_raw = [place(f"mat_raw{n}", [P, PACK, b - a], F32) for n, (a, b) in enumerate(MAT_CHUNKS)]
        anchors = [place(f"anchor{c}", [P, U], F32) for c in range(D_TILES)]
        olds = [place(f"old{c}", [P, T], F32) for c in range(D_TILES)]
        windows = [place(f"window{c}", [P, T], F32) for c in range(4)]
        ident = place("ident", [P, P], F32)

        nc.vector.memset(scale_bytes[:].bitcast(I32), 0)
        mat_rows = mat.rearrange("(p j) d -> p j d", j=PACK)

        def load_mat(n):
            nc.sync.dma_start(mat_raw[n][:], mat_rows[:, :, MAT_CHUNKS[n][0] : MAT_CHUNKS[n][1]])

        def load_anchor(c):
            nc.sync.dma_start(anchors[c][:], anchor[rows(c), :])

        def load_old(c):
            nc.sync.dma_start(olds[c][:], old[rows(c), :])

        nc.sync.dma_start(offsets[:], offs)
        nc.sync.dma_start(pull_cols[:], pull[0].rearrange("(p j) -> p j", j=2))
        nc.sync.dma_start(offsets2[:], offs2)
        load_anchor(0)
        load_mat(0)
        nc.sync.dma_start(words[:].bitcast(I32), tab_words[0].rearrange("p n t -> p (n t)").bitcast(I32))
        for q in range(4):
            nc.sync.dma_start(scale_bytes[32 * q : 32 * q + 4, :].bitcast(I32), tab_scales[0, 4 * q : 4 * q + 4, :].bitcast(I32))
        nc.sync.dma_start(coef_cols[:], coef[0].rearrange("(p j) -> p j", j=2))
        load_mat(1)
        load_anchor(1)
        load_old(0)
        load_mat(2)
        load_old(1)
        load_anchor(2)
        load_anchor(3)
        load_old(2)
        load_old(3)

        make_identity(nc, ident[:])
        for c in range(len(windows)):
            (nc.vector if c < 2 else nc.gpsimd).memset(windows[c][:], 0.0)

        def spread(cols, name, copy):
            bank = psum.tile([P, 2, P], F32, name=name + "_bank", tag=BANKS[name])
            for j in range(2):
                nc.tensor.transpose(bank[:, j, :], cols[:, j : j + 1].to_broadcast([P, P]), ident[:])
            row = place(name + "_row", [P, I], F32)
            copy(row[:].rearrange("p (n j) -> p n j", j=2), bank[:].rearrange("p j n -> p n j"))
            return row

        pull_row = spread(pull_cols, "pull", nc.vector.tensor_copy)
        coef_row = spread(coef_cols, "coef", nc.scalar.copy)

        picked_words = place("picked_words", [P, I], U32)
        picked_scales = place("picked_scales", [P, I], U8)
        pulled, weighted, stationary, products, turned_banks, results = {}, {}, {}, {}, {}, {}

        def quantise(n):
            a, b = MAT_CHUNKS[n]
            grouped = place(f"grouped{n}", [P, b - a, PACK], BF16)
            nc.scalar.copy(
                grouped[:].rearrange("p (c i) t -> p c t i", i=4),
                mat_raw[n][:].rearrange("p t (c i) -> p c t i", i=4),
            )
            codes = place(f"codes{n}", [P, b - a], U32)
            scales = place(f"scales{n}", [P, b - a], U8)
            nc.vector.quantize_mx(out=codes[:].bitcast(FP8X4), scales=scales[:], in_=grouped[:].rearrange("p w t -> p (w t)"))
            for c in range(a // P, b // P):
                cols = slice(c * P - a, (c + 1) * P - a)
                products[c] = psum.tile([P, I], F32, name=f"z{c}", tag=BANKS[f"z{c}"])
                nc.tensor.matmul_mx(
                    out=products[c][:],
                    lhsT=codes[:, cols].bitcast(FP8X4),
                    lhsT_scale=scales[:, cols],
                    rhs=picked_words[:].bitcast(FP8X4),
                    rhs_scale=picked_scales[:],
                    start=True,
                    stop=True,
                )

        def gather_anchor(c):
            pulled[c] = place(f"pulled{c}", [P, I], F32)
            nc.vector.tensor_tensor(pulled[c][:], anchors[c][:].indirect(offsets2[:]), pull_row[:], MULT)

        def weigh(c):
            weighted[c] = place(f"weighted{c}", [P, I], F32)
            nc.vector.tensor_tensor(weighted[c][:], products[c][:], coef_row[:], MULT)

        def scatter(c):
            nc.vector.tensor_tensor(windows[c % len(windows)][:].indirect(offsets[:]), weighted[c][:], pulled[c][:], ADD)

        def add_on_vector(c, s):
            nc.vector.tensor_tensor(olds[c][:, half(s)], olds[c][:, half(s)], windows[c % len(windows)][:, half(s)], ADD)
            nc.sync.dma_start(out[rows(c), half(s)], olds[c][:, half(s)])

        def turn_old(c, s):
            bank = psum.tile([P, BLOCKS, P], F32, name=f"turned{c}{s}", tag=BANKS[f"turned{c}{s}"])
            turned_banks[c, s] = bank
            for j in range(BLOCKS):
                nc.tensor.matmul(bank[:, j, :], olds[c][:, rows(BLOCKS * s + j)], ident[:], start=(j == 0), stop=False, is_transpose=True)

        def add_on_tensor(c, s):
            bank = turned_banks[c, s]
            for j in range(BLOCKS):
                nc.tensor.matmul(bank[:, j, :], windows[c][:, rows(BLOCKS * s + j)], ident[:], start=False, stop=(j == BLOCKS - 1), is_transpose=True)
            turned = place(f"turned_sum{c}{s}", [P, BLOCKS, P], F32)
            nc.scalar.copy(turned[:], bank[:])
            back = psum.tile([P, BLOCKS, P], F32, name=f"back{c}{s}", tag=BANKS[f"back{c}{s}"])
            for j in range(BLOCKS):
                nc.tensor.transpose(back[:, j, :], turned[:, j, :], ident[:])
            result = place(f"result{c}{s}", [P, BLOCKS, P], F32)
            nc.scalar.copy(result[:], back[:])
            results[c, s] = result
            nc.scalar.dma_start(out[rows(c), half(s)], result[:].rearrange("p j n -> p (j n)"))

        gather_anchor(0)
        nc.vector.tensor_copy(picked_words[:], words[:].indirect(offsets[:]))
        nc.vector.tensor_copy(picked_scales[:], scale_bytes[:].indirect(offsets[:]))
        quantise(0)
        gather_anchor(1)
        quantise(1)
        weigh(0)
        weigh(1)
        turn_old(0, 0)
        turn_old(0, 1)
        scatter(0)
        scatter(1)
        quantise(2)
        add_on_tensor(0, 0)
        add_on_tensor(0, 1)
        gather_anchor(2)
        gather_anchor(3)
        weigh(2)
        weigh(3)
        scatter(2)
        turn_old(1, 0)
        add_on_tensor(1, 0)
        turn_old(1, 1)
        add_on_tensor(1, 1)
        scatter(3)
        add_on_vector(2, 0)
        add_on_vector(2, 1)
        add_on_vector(3, 0)
        add_on_vector(3, 1)
